import numpy as np
import ml_dtypes


def mxq(x, axis, fmt="e4m3"):
    dtype, down = {"e4m3": (ml_dtypes.float8_e4m3fn, 7), "e5m2": (ml_dtypes.float8_e5m2, 14)}[fmt]
    v = np.moveaxis(np.asarray(x, np.float32).astype(ml_dtypes.bfloat16).astype(np.float64), axis, -1)
    blocks = v.reshape(v.shape[:-1] + (-1, 32))
    amax = np.abs(blocks).max(-1, keepdims=True)
    byte = np.maximum(np.where(amax > 0, np.frexp(amax)[1] - 1 + 127, 0) - down, 1)
    scale = np.exp2(byte - 127.0)
    codes = (blocks / scale).astype(np.float32).astype(dtype).astype(np.float64)
    return np.moveaxis((codes * scale).reshape(v.shape), -1, axis)


WIDE = False


def mx_kscale(k):
    if not WIDE:
        return np.ones(k)
    levels = np.array([10, -10, 5, -5, 0])
    if k % 512:
        return np.exp2(np.random.permutation(np.resize(levels, k // 32))).repeat(32)
    a = np.empty((k // 512, 16))
    for p in range(k // 512):
        a[p, :8] = np.random.permutation(np.resize(levels, 8))
        for g in range(8):
            far = levels[np.abs(levels - a[p, g]) >= 10]
            a[p, g + 8] = far[np.random.randint(len(far))]
    return np.exp2(a.ravel()).repeat(32)


def f64(x):
    return np.asarray(x).astype(np.float64)


def striped8(idx):
    return np.concatenate([x.reshape(-1, 16).T for x in idx]).astype(np.uint16)


def runs(offs, k):
    lists = np.stack([offs[16 * r : 16 * r + 16].T.reshape(-1) for r in range(8)]).astype(np.int64)
    return lists[np.arange(k) % 512 // 64]


def pack_weight(w):
    k, n = w.shape
    w = f64(np.asarray(w, np.float32).astype(ml_dtypes.bfloat16)).reshape(k // 32, 32, n)
    amax = np.abs(w).max(1)
    byte = np.clip(np.where(amax > 0, np.frexp(amax)[1] - 1 + 127 - 7, 1), 1, 254)
    scaled = (w * np.exp2(127.0 - byte)[:, None, :]).reshape(k, n).astype(np.float32)
    words = np.ascontiguousarray(scaled.reshape(k // 512, 128, 4, n).transpose(0, 1, 3, 2)).astype(ml_dtypes.float8_e4m3fn).view(np.uint8)
    return words, np.ascontiguousarray(byte.astype(np.uint8).reshape(k // 512, 16, n))


def unpack_weight(words, scales):
    g, p, n, _ = words.shape
    vals = np.ascontiguousarray(words).view(ml_dtypes.float8_e4m3fn).astype(np.float64) * np.repeat(np.exp2(scales.astype(np.float64) - 127.0), 8, axis=1)[..., None]
    return vals.transpose(0, 1, 3, 2).reshape(g * 512, n)

def planes(y):
    n, m = y.shape
    v = y.astype(np.float32).astype(ml_dtypes.bfloat16).astype(np.float64).reshape(n // 32, 32, m)
    top = np.abs(v).max(1)
    byte = np.clip(np.where(top > 0, np.frexp(top)[1] - 1 + 127 - 7, 1), 1, 254)
    codes = (v * np.exp2(127.0 - byte)[:, None, :]).reshape(n, m).astype(np.float32).astype(ml_dtypes.float8_e4m3fn).view(np.uint8)
    words = codes.reshape(n // 512, 128, 4, m).transpose(0, 1, 3, 2)
    return np.ascontiguousarray(words), np.ascontiguousarray(byte.astype(np.uint8).reshape(n // 512, 16, m))


K, T, S, H = 512, 2048, 512, 512


def setup_inputs():
    n = np.random.standard_normal
    s = mx_kscale(K)[:, None]
    u = mx_kscale(H)
    packed_xT = pack_weight(n((K, T)) * s)
    packed_w1 = pack_weight(n((K, H)) / np.sqrt(K) / s)
    packed_w2 = pack_weight(n((H, H)) / np.sqrt(H) / u[:, None])
    packed_w3 = pack_weight(n((H, H)) / np.sqrt(H) / u[:, None])
    return {
        "x_words": packed_xT[0],
        "x_scales": packed_xT[1],
        "w1_words": packed_w1[0],
        "w1_scales": packed_w1[1],
        "gn": (np.random.uniform(0.5, 1.5, (H, 1)) * u[:, None]).astype(np.float32),
        "w2_words": packed_w2[0],
        "w2_scales": packed_w2[1],
        "w3_words": packed_w3[0],
        "w3_scales": packed_w3[1],
        "offs": striped8(np.stack([np.random.permutation(T)[:S] for _ in range(8)])),
        "pair": striped8(np.stack([np.random.permutation(S) for _ in range(8)])),
    }


def reference(x_words, x_scales, w1_words, w1_scales, gn, w2_words, w2_scales, w3_words, w3_scales, offs, pair):
    xq = unpack_weight(x_words, x_scales)[np.arange(K)[:, None], runs(offs, K)]
    y = unpack_weight(w1_words, w1_scales).T @ xq
    z = f64(gn) * y
    x1 = y + y * (0.5 * ((unpack_weight(w2_words, w2_scales).T @ mxq(z, 0, "e4m3"))))
    z2 = f64(gn) * (x1[np.arange(H)[:, None], runs(pair, H)])
    out_0 = x1 + y * (0.5 * ((unpack_weight(w3_words, w3_scales).T @ mxq(z2, 0, "e4m3"))))
    return (out_0,) + planes(out_0)

@@ -1,0 +1,201 @@
+from contextlib import ExitStack
+
+import concourse.mybir as mybir
+
+F32 = mybir.dt.float32
+BF16 = mybir.dt.bfloat16
+I32 = mybir.dt.int32
+U32 = mybir.dt.uint32
+U16 = mybir.dt.uint16
+U8 = mybir.dt.uint8
+FP8X4 = mybir.dt.float8_e4m3fn_x4
+ADD = mybir.AluOpType.add
+MULT = mybir.AluOpType.mult
+COPY = mybir.ActivationFunctionType.Copy
+
+P = 128
+PACK = 4
+T, S, H = 2048, 512, 512
+HALF = 256
+CH = 128
+FLOPS = 3 * 2 * 512 * 512 * 512
+
+
+def tile_picked_dcn2_none_po_kernel(
+    tc, x_words, x_scales, w1_words, w1_scales, gn, w2_words, w2_scales, w3_words, w3_scales, offs, pair, out_0, out_1, out_2
+):
+    nc = tc.nc
+
+    def words_of(ap):
+        return ap[0].rearrange("p n t -> p (n t)").bitcast(I32)
+
+    def deal(dst, src):
+        nc.vector.tensor_copy(out=dst.rearrange("p (t m) -> p m t", t=PACK), in_=src.rearrange("p (m t) -> p m t", t=PACK))
+
+    with ExitStack() as ctx:
+        keep = ctx.enter_context(tc.tile_pool(name="keep", bufs=1))
+        ring = ctx.enter_context(tc.tile_pool(name="ring", bufs=3))
+        psum = ctx.enter_context(tc.psum_pool(name="psum", bufs=1))
+
+        offs_t = keep.tile([P, S // 16], U16, name="offs_t")
+        pair_t = keep.tile([P, S // 16], U16, name="pair_t")
+        xs_all = keep.tile([P, T], U8, name="xs_all", tag="xs_all", align_bytes=64)
+        xw_all = keep.tile([P, T], U32, name="xw_all", tag="xw_all", align_bytes=64)
+        xs_got = keep.tile([P, S], U8, name="xs_got", align_bytes=64)
+        xs = keep.tile([P, S], U8, name="xs", align_bytes=64)
+        xw = keep.tile([P, S], U32, name="xw", align_bytes=64)
+        raw_w = [keep.tile([P, H], I32, name="raw_w%d" % i, align_bytes=64) for i in range(2)]
+        w = [keep.tile([P, H], I32, name="w%d" % i, align_bytes=64) for i in range(3)]
+        raw_s1 = keep.tile([P, H], U8, name="raw_s1", align_bytes=64)
+        s1 = keep.tile([P, H], U8, name="s1", align_bytes=64)
+        s23 = keep.tile([P, H], U8, name="s23", align_bytes=64)
+        gain = keep.tile([P, PACK], F32, name="gain")
+        half_gain = keep.tile([P, PACK], F32, name="half_gain")
+
+        nc.gpsimd.memset(raw_s1[:].bitcast(I32), 0)
+        nc.vector.memset(xs_all[:].bitcast(I32), 0)
+        nc.vector.memset(xs[:].bitcast(I32), 0)
+
+        nc.sync.dma_start(offs_t[:], offs)
+        nc.sync.dma_start(raw_w[0][:], words_of(w1_words))
+        for q in range(4):
+            nc.scalar.dma_start(raw_s1[32 * q : 32 * q + 4, :].bitcast(I32), w1_scales[0, 4 * q : 4 * q + 4, :].bitcast(I32))
+        nc.sync.dma_start(xs_all[0:P:8, :].bitcast(I32), x_scales[0].bitcast(I32))
+        nc.sync.dma_start(xw_all[:].bitcast(I32), words_of(x_words))
+        nc.gpsimd.dma_start(gain[:], gn.rearrange("(p t) o -> p (t o)", t=PACK))
+        nc.sync.dma_start(pair_t[:], pair)
+        nc.sync.dma_start(raw_w[1][:], words_of(w2_words))
+        nc.scalar.activation(half_gain[:], gain[:], COPY, scale=0.5)
+
+        nc.vector.tensor_copy(out=xs_got[:], in_=xs_all[:].indirect(offs_t[:]))
+        for r in range(4):
+            nc.scalar.dma_start(xs[r:P:32, :].bitcast(I32), xs_got[8 * r : P : 32, :].bitcast(I32))
+        raw_s23 = keep.tile([P, H], U8, name="raw_s23", tag="xs_all", align_bytes=64)
+        nc.vector.memset(raw_s23[:].bitcast(I32), 0)
+        for i, src in enumerate((w2_scales, w3_scales)):
+            for q in range(4):
+                row = 32 * q + 4 * i
+                nc.sync.dma_start(raw_s23[row : row + 4, :].bitcast(I32), src[0, 4 * q : 4 * q + 4, :].bitcast(I32))
+
+        deal(w[0][:], raw_w[0][:])
+        deal(s1[:], raw_s1[:])
+
+        def mm(out, i, t, rhs, rhs_scale, start=True, stop=True):
+            cols = slice(P * t, P * (t + 1))
+            plane = s1[:, cols] if i == 0 else s23[4 * (i - 1) : P, cols]
+            nc.tensor.matmul_mx(out=out, lhsT=w[i][:, cols].bitcast(FP8X4), lhsT_scale=plane,
+                                rhs=rhs.bitcast(FP8X4), rhs_scale=rhs_scale, start=start, stop=stop)
+
+        halves = [slice(h * HALF, (h + 1) * HALF) for h in range(2)]
+        y_ps = [[psum.tile([P, 2, HALF], F32, name="y_ps", tag="b%d" % (2 * h + u)) for u in range(2)] for h in range(2)]
+        zh = keep.tile([P, PACK, S], F32, name="zh")
+        yh = keep.tile([P, PACK, S], F32, name="yh")
+        z_bf = keep.tile([P, S, PACK], BF16, name="z_bf", align_bytes=64)
+        z_w = keep.tile([P, S], U32, name="z_w", align_bytes=64)
+        z_s = keep.tile([P, S], U8, name="z_s", align_bytes=64)
+
+        for h in range(2):
+            nc.vector.tensor_copy(out=xw[:, halves[h]], in_=xw_all[:].indirect(offs_t[:, 16 * h : 16 * (h + 1)]))
+            for t in range(PACK):
+                mm(y_ps[h][t // 2][:, t % 2, :], 0, t, xw[:, halves[h]], xs[:, halves[h]])
+        raw_w3 = keep.tile([P, H], I32, name="raw_w3", tag="xw_all", align_bytes=64)
+        nc.sync.dma_start(raw_w3[:], words_of(w3_words))
+        deal(w[1][:], raw_w[1][:])
+        deal(s23[:], raw_s23[:])
+        for h in range(2):
+            for t in range(PACK):
+                src = y_ps[h][t // 2][:, t % 2, :]
+                nc.scalar.activation(zh[:, t, halves[h]], src, COPY, scale=half_gain[:, t : t + 1])
+        for h in range(2):
+            for u in range(2):
+                nc.scalar.activation(yh[:, 2 * u : 2 * u + 2, halves[h]], y_ps[h][u][:], COPY, scale=0.5)
+        deal(w[2][:], raw_w3[:])
+
+        m2_ps = [[psum.tile([P, 2, HALF], F32, name="m2_ps", tag="b%d" % (4 + 2 * h + u)) for u in range(2)] for h in range(2)]
+        win = [keep.tile([P, S], F32, name="win%d" % t) for t in range(PACK)]
+        s0 = keep.tile([P, PACK, CH], F32, name="s0")
+        for h in range(2):
+            nc.vector.tensor_scalar(out=z_bf[:, halves[h], :], in0=zh[:, :, halves[h]].rearrange("p t j -> p j t"),
+                                    scalar1=2.0, scalar2=None, op0=MULT)
+            nc.vector.quantize_mx(out=z_w[:, halves[h]].bitcast(FP8X4), scales=z_s[:, halves[h]],
+                                  in_=z_bf[:, halves[h], :].rearrange("p j t -> p (j t)"))
+            for t in range(PACK):
+                mm(m2_ps[h][t // 2][:, t % 2, :], 1, t, z_w[:, halves[h]], z_s[:, halves[h]])
+        for h in range(2):
+            for t in range(PACK):
+                nc.vector.scalar_tensor_tensor(out=win[t][:, halves[h]], in0=m2_ps[h][t // 2][:, t % 2, :], scalar=2.0,
+                                               in1=zh[:, t, halves[h]], op0=ADD, op1=MULT)
+        for u in range(2):
+            nc.scalar.activation(s0[:, 2 * u : 2 * u + 2, :], m2_ps[0][u][:, :, 0:CH], COPY, bias=2.0)
+
+        n_ch = S // CH
+        o_w = keep.tile([P, S], U32, name="o_w", align_bytes=64)
+        o_s = keep.tile([P, S], U8, name="o_s", align_bytes=64)
+        out_rows = out_0.rearrange("(p t) j -> p t j", t=PACK)
+        out_words = words_of(out_1)
+        woven, banks, res = {}, {}, {}
+
+        def weave(c, dst, src):
+            if c == n_ch - 1:
+                nc.vector.tensor_copy(out=dst, in_=src.rearrange("p t j -> p j t"))
+            else:
+                nc.scalar.copy(out=dst, in_=src.rearrange("p t j -> p j t"))
+
+        def fetch(c):
+            got = ring.tile([P, PACK, CH], BF16, name="got", tag="stage", align_bytes=64)
+            for t in range(PACK):
+                nc.vector.tensor_copy(out=got[:, t, :], in_=win[t][:].indirect(pair_t[:, 8 * c : 8 * (c + 1)]))
+            woven[c] = ring.tile([P, CH, PACK], BF16, name="woven", tag="stage", align_bytes=64)
+            weave(c, woven[c][:], got[:])
+
+        def product(c):
+            cols = slice(c * CH, (c + 1) * CH)
+            z2_w = keep.tile([P, CH], U32, name="z2_w%d" % c, align_bytes=64)
+            z2_s = keep.tile([P, CH], U8, name="z2_s%d" % c, align_bytes=64)
+            nc.vector.quantize_mx(out=z2_w[:].bitcast(FP8X4), scales=z2_s[:], in_=woven[c][:].rearrange("p j t -> p (j t)"))
+            if c == n_ch - 1:
+                banks[c] = [psum.tile([P, CH], F32, name="last", tag="b%d" % (4 + t))[:] for t in range(PACK)]
+                for t in range(PACK):
+                    mm(banks[c][t], 1, t, z_w[:, cols], z_s[:, cols], stop=False)
+                for t in range(PACK):
+                    mm(banks[c][t], 2, t, z2_w[:], z2_s[:], start=False)
+            else:
+                banks[c] = psum.tile([P, PACK, CH], F32, name="m3", tag="b%d" % c)
+                for t in range(PACK):
+                    if c > 0:
+                        mm(banks[c][:, t, :], 1, t, z_w[:, cols], z_s[:, cols], stop=False)
+                    mm(banks[c][:, t, :], 2, t, z2_w[:], z2_s[:], start=(c == 0))
+
+        def finish(c):
+            cols = slice(c * CH, (c + 1) * CH)
+            res[c] = keep.tile([P, PACK, CH], F32, name="res%d" % c)
+            if c == 0:
+                both = keep.tile([P, PACK, CH], F32, name="both")
+                nc.vector.tensor_tensor(out=both[:], in0=banks[c][:], in1=s0[:], op=ADD)
+                nc.vector.tensor_tensor(out=res[c][:], in0=both[:], in1=yh[:, :, cols], op=MULT)
+            elif c == n_ch - 1:
+                for t in range(PACK):
+                    nc.vector.scalar_tensor_tensor(out=res[c][:, t, :], in0=banks[c][t], scalar=2.0, in1=yh[:, t, cols], op0=ADD, op1=MULT)
+            else:
+                nc.vector.scalar_tensor_tensor(out=res[c][:], in0=banks[c][:], scalar=2.0, in1=yh[:, :, cols], op0=ADD, op1=MULT)
+            nc.sync.dma_start(out_rows[:, :, cols], res[c][:])
+
+        def hand_on(c):
+            cols = slice(c * CH, (c + 1) * CH)
+            o_bf = keep.tile([P, CH, PACK], BF16, name="o_bf%d" % c, align_bytes=64)
+            weave(c, o_bf[:], res[c][:])
+            nc.vector.quantize_mx(out=o_w[:, cols].bitcast(FP8X4), scales=o_s[:, cols], in_=o_bf[:].rearrange("p j t -> p (j t)"))
+            nc.sync.dma_start(out_words[:, cols], o_w[:, cols].bitcast(I32))
+
+        for step in range(n_ch + 3):
+            if step < n_ch:
+                fetch(step)
+            if 0 <= step - 1 < n_ch:
+                product(step - 1)
+            if 0 <= step - 2 < n_ch:
+                finish(step - 2)
+            if 0 <= step - 3 < n_ch:
+                hand_on(step - 3)
+        for q in range(4):
+            queue = nc.scalar if q % 2 else nc.sync
+            queue.dma_start(out_2[0, 4 * q : 4 * q + 4, :].bitcast(I32), o_s[32 * q : 32 * q + 4, :].bitcast(I32))

@@ -29,39 +29,40 @@ def tile_picked_dcn2_none_po_kernel(
     def words_of(ap):
         return ap[0].rearrange("p n t -> p (n t)").bitcast(I32)
 
-    def deal(dst, src):
-        nc.vector.tensor_copy(out=dst.rearrange("p (t m) -> p m t", t=PACK), in_=src.rearrange("p (m t) -> p m t", t=PACK))
+    def deal(dst, src, run):
+        nc.vector.tensor_copy(out=dst.rearrange("p (t m i) -> p m t i", t=PACK, i=run), in_=src.rearrange("p (m i t) -> p m t i", t=PACK, i=run))
 
     with ExitStack() as ctx:
         keep = ctx.enter_context(tc.tile_pool(name="keep", bufs=1))
-        ring = ctx.enter_context(tc.tile_pool(name="ring", bufs=3))
         psum = ctx.enter_context(tc.psum_pool(name="psum", bufs=1))
 
         offs_t = keep.tile([P, S // 16], U16, name="offs_t")
         pair_t = keep.tile([P, S // 16], U16, name="pair_t")
         xs_all = keep.tile([P, T], U8, name="xs_all", tag="xs_all", align_bytes=64)
         xw_all = keep.tile([P, T], U32, name="xw_all", tag="xw_all", align_bytes=64)
-        xs_got = keep.tile([P, S], U8, name="xs_got", align_bytes=64)
+        xs_got = keep.tile([P, S], U8, name="xs_got", tag="xs_got", align_bytes=64)
         xs = keep.tile([P, S], U8, name="xs", align_bytes=64)
         xw = keep.tile([P, S], U32, name="xw", align_bytes=64)
-        raw_w = [keep.tile([P, H], I32, name="raw_w%d" % i, align_bytes=64) for i in range(2)]
-        w = [keep.tile([P, H], I32, name="w%d" % i, align_bytes=64) for i in range(3)]
+        raw_w = [keep.tile([P, H], I32, name="raw_w%d" % i, tag="raw_w%d" % i, align_bytes=64) for i in range(2)]
+        w = {2: keep.tile([P, H], I32, name="w2", align_bytes=64)}
         raw_s1 = keep.tile([P, H], U8, name="raw_s1", align_bytes=64)
-        s1 = keep.tile([P, H], U8, name="s1", align_bytes=64)
-        s23 = keep.tile([P, H], U8, name="s23", align_bytes=64)
-        gain = keep.tile([P, PACK], F32, name="gain")
         half_gain = keep.tile([P, PACK], F32, name="half_gain")
+        planes = [keep.tile([P, H], U8, name="plane%d" % i, align_bytes=64) for i in range(3)]
+        gain = keep.tile([P, PACK], F32, name="gain")
 
-        nc.gpsimd.memset(raw_s1[:].bitcast(I32), 0)
         nc.vector.memset(xs_all[:].bitcast(I32), 0)
+        nc.gpsimd.memset(raw_s1[:].bitcast(I32), 0)
         nc.vector.memset(xs[:].bitcast(I32), 0)
 
+        def load_scale_rows(queue, dst, src):
+            for q in range(4):
+                queue.dma_start(dst[32 * q : 32 * q + 4, :].bitcast(I32), src[0, 4 * q : 4 * q + 4, :].bitcast(I32))
+
         nc.sync.dma_start(offs_t[:], offs)
-        nc.sync.dma_start(raw_w[0][:], words_of(w1_words))
-        for q in range(4):
-            nc.scalar.dma_start(raw_s1[32 * q : 32 * q + 4, :].bitcast(I32), w1_scales[0, 4 * q : 4 * q + 4, :].bitcast(I32))
         nc.sync.dma_start(xs_all[0:P:8, :].bitcast(I32), x_scales[0].bitcast(I32))
+        nc.sync.dma_start(raw_w[0][:], words_of(w1_words))
         nc.sync.dma_start(xw_all[:].bitcast(I32), words_of(x_words))
+        load_scale_rows(nc.scalar, raw_s1, w1_scales)
         nc.gpsimd.dma_start(gain[:], gn.rearrange("(p t) o -> p (t o)", t=PACK))
         nc.sync.dma_start(pair_t[:], pair)
         nc.sync.dma_start(raw_w[1][:], words_of(w2_words))
@@ -69,28 +70,26 @@ def tile_picked_dcn2_none_po_kernel(
 
         nc.vector.tensor_copy(out=xs_got[:], in_=xs_all[:].indirect(offs_t[:]))
         for r in range(4):
-            nc.scalar.dma_start(xs[r:P:32, :].bitcast(I32), xs_got[8 * r : P : 32, :].bitcast(I32))
-        raw_s23 = keep.tile([P, H], U8, name="raw_s23", tag="xs_all", align_bytes=64)
-        nc.vector.memset(raw_s23[:].bitcast(I32), 0)
-        for i, src in enumerate((w2_scales, w3_scales)):
-            for q in range(4):
-                row = 32 * q + 4 * i
-                nc.sync.dma_start(raw_s23[row : row + 4, :].bitcast(I32), src[0, 4 * q : 4 * q + 4, :].bitcast(I32))
-
-        deal(w[0][:], raw_w[0][:])
-        deal(s1[:], raw_s1[:])
+            nc.sync.dma_start(xs[r:P:32, :].bitcast(I32), xs_got[8 * r : P : 32, :].bitcast(I32))
+        w[0] = keep.tile([P, H], I32, name="w0", tag="xs_all", align_bytes=64)
+        deal(w[0][:], raw_w[0][:], 4)
+        raw_s2 = keep.tile([P, H], U8, name="raw_s2", tag="raw_w0", align_bytes=64)
+        nc.vector.memset(raw_s2[:].bitcast(I32), 0)
+        load_scale_rows(nc.sync, raw_s2, w2_scales)
+        raw_w3 = keep.tile([P, H], I32, name="raw_w3", tag="xs_got", align_bytes=64)
+        nc.sync.dma_start(raw_w3[:], words_of(w3_words))
+        deal(planes[0][:], raw_s1[:], 16)
+        halves = [slice(h * HALF, (h + 1) * HALF) for h in range(2)]
 
         def mm(out, i, t, rhs, rhs_scale, start=True, stop=True):
             cols = slice(P * t, P * (t + 1))
-            plane = s1[:, cols] if i == 0 else s23[4 * (i - 1) : P, cols]
+            plane = planes[i][:, cols]
             nc.tensor.matmul_mx(out=out, lhsT=w[i][:, cols].bitcast(FP8X4), lhsT_scale=plane,
                                 rhs=rhs.bitcast(FP8X4), rhs_scale=rhs_scale, start=start, stop=stop)
 
-        halves = [slice(h * HALF, (h + 1) * HALF) for h in range(2)]
         y_ps = [[psum.tile([P, 2, HALF], F32, name="y_ps", tag="b%d" % (2 * h + u)) for u in range(2)] for h in range(2)]
         zh = keep.tile([P, PACK, S], F32, name="zh")
-        yh = keep.tile([P, PACK, S], F32, name="yh")
-        z_bf = keep.tile([P, S, PACK], BF16, name="z_bf", align_bytes=64)
+        z_bf = keep.tile([P, S, PACK], BF16, name="z_bf", tag="z_bf", align_bytes=64)
         z_w = keep.tile([P, S], U32, name="z_w", align_bytes=64)
         z_s = keep.tile([P, S], U8, name="z_s", align_bytes=64)
 
@@ -98,25 +97,29 @@ def tile_picked_dcn2_none_po_kernel(
             nc.vector.tensor_copy(out=xw[:, halves[h]], in_=xw_all[:].indirect(offs_t[:, 16 * h : 16 * (h + 1)]))
             for t in range(PACK):
                 mm(y_ps[h][t // 2][:, t % 2, :], 0, t, xw[:, halves[h]], xs[:, halves[h]])
-        raw_w3 = keep.tile([P, H], I32, name="raw_w3", tag="xw_all", align_bytes=64)
-        nc.sync.dma_start(raw_w3[:], words_of(w3_words))
-        deal(w[1][:], raw_w[1][:])
-        deal(s23[:], raw_s23[:])
+        w[1] = keep.tile([P, H], I32, name="w1", tag="xw_all", align_bytes=64)
+        deal(w[1][:], raw_w[1][:], 4)
+        raw_s3 = keep.tile([P, H], U8, name="raw_s3", tag="raw_w1", align_bytes=64)
+        nc.vector.memset(raw_s3[:].bitcast(I32), 0)
+        load_scale_rows(nc.sync, raw_s3, w3_scales)
+        deal(planes[1][:], raw_s2[:], 16)
         for h in range(2):
             for t in range(PACK):
                 src = y_ps[h][t // 2][:, t % 2, :]
                 nc.scalar.activation(zh[:, t, halves[h]], src, COPY, scale=half_gain[:, t : t + 1])
-        for h in range(2):
-            for u in range(2):
-                nc.scalar.activation(yh[:, 2 * u : 2 * u + 2, halves[h]], y_ps[h][u][:], COPY, scale=0.5)
-        deal(w[2][:], raw_w3[:])
+        deal(w[2][:], raw_w3[:], 4)
+        deal(planes[2][:], raw_s3[:], 16)
 
         m2_ps = [[psum.tile([P, 2, HALF], F32, name="m2_ps", tag="b%d" % (4 + 2 * h + u)) for u in range(2)] for h in range(2)]
         win = [keep.tile([P, S], F32, name="win%d" % t) for t in range(PACK)]
         s0 = keep.tile([P, PACK, CH], F32, name="s0")
         for h in range(2):
-            nc.vector.tensor_scalar(out=z_bf[:, halves[h], :], in0=zh[:, :, halves[h]].rearrange("p t j -> p j t"),
+            on_vector = halves[h] if h == 0 else slice(HALF, HALF + CH)
+            nc.vector.tensor_scalar(out=z_bf[:, on_vector, :].rearrange("p (c i) t -> p c t i", i=4), in0=zh[:, :, on_vector].rearrange("p t (c i) -> p c t i", i=4),
                                     scalar1=2.0, scalar2=None, op0=MULT)
+            if h == 1:
+                nc.scalar.activation(z_bf[:, HALF + CH : S, :].rearrange("p (c i) t -> p c t i", i=4),
+                                     zh[:, :, HALF + CH : S].rearrange("p t (c i) -> p c t i", i=4), COPY, scale=2.0)
             nc.vector.quantize_mx(out=z_w[:, halves[h]].bitcast(FP8X4), scales=z_s[:, halves[h]],
                                   in_=z_bf[:, halves[h], :].rearrange("p j t -> p (j t)"))
             for t in range(PACK):
@@ -127,75 +130,76 @@ def tile_picked_dcn2_none_po_kernel(
                                                in1=zh[:, t, halves[h]], op0=ADD, op1=MULT)
         for u in range(2):
             nc.scalar.activation(s0[:, 2 * u : 2 * u + 2, :], m2_ps[0][u][:, :, 0:CH], COPY, bias=2.0)
+        yh = keep.tile([P, PACK, S], F32, name="yh", tag="z_bf", align_bytes=64)
+        for h in range(2):
+            for u in range(2):
+                nc.scalar.activation(yh[:, 2 * u : 2 * u + 2, halves[h]], y_ps[h][u][:], COPY, scale=0.5)
 
         n_ch = S // CH
         o_w = keep.tile([P, S], U32, name="o_w", align_bytes=64)
         o_s = keep.tile([P, S], U8, name="o_s", align_bytes=64)
         out_rows = out_0.rearrange("(p t) j -> p t j", t=PACK)
         out_words = words_of(out_1)
-        woven, banks, res = {}, {}, {}
+        chunks = [slice(c * CH, (c + 1) * CH) for c in range(n_ch)]
+        z2_w = keep.tile([P, S], U32, name="z2_w", align_bytes=64)
+        z2_s = keep.tile([P, S], U8, name="z2_s", align_bytes=64)
 
-        def weave(c, dst, src):
-            if c == n_ch - 1:
-                nc.vector.tensor_copy(out=dst, in_=src.rearrange("p t j -> p j t"))
-            else:
-                nc.scalar.copy(out=dst, in_=src.rearrange("p t j -> p j t"))
+        def weave(copy, dst, src):
+            copy(out=dst.rearrange("p (c i) t -> p c t i", i=4), in_=src.rearrange("p t (c i) -> p c t i", i=4))
 
-        def fetch(c):
-            got = ring.tile([P, PACK, CH], BF16, name="got", tag="stage", align_bytes=64)
+        def fetch(got, cols):
             for t in range(PACK):
-                nc.vector.tensor_copy(out=got[:, t, :], in_=win[t][:].indirect(pair_t[:, 8 * c : 8 * (c + 1)]))
-            woven[c] = ring.tile([P, CH, PACK], BF16, name="woven", tag="stage", align_bytes=64)
-            weave(c, woven[c][:], got[:])
+                nc.vector.tensor_copy(out=got[:, t, :], in_=win[t][:].indirect(pair_t[:, cols.start // 16 : cols.stop // 16]))
 
-        def product(c):
-            cols = slice(c * CH, (c + 1) * CH)
-            z2_w = keep.tile([P, CH], U32, name="z2_w%d" % c, align_bytes=64)
-            z2_s = keep.tile([P, CH], U8, name="z2_s%d" % c, align_bytes=64)
-            nc.vector.quantize_mx(out=z2_w[:].bitcast(FP8X4), scales=z2_s[:], in_=woven[c][:].rearrange("p j t -> p (j t)"))
-            if c == n_ch - 1:
-                banks[c] = [psum.tile([P, CH], F32, name="last", tag="b%d" % (4 + t))[:] for t in range(PACK)]
-                for t in range(PACK):
-                    mm(banks[c][t], 1, t, z_w[:, cols], z_s[:, cols], stop=False)
-                for t in range(PACK):
-                    mm(banks[c][t], 2, t, z2_w[:], z2_s[:], start=False)
-            else:
-                banks[c] = psum.tile([P, PACK, CH], F32, name="m3", tag="b%d" % c)
-                for t in range(PACK):
-                    if c > 0:
-                        mm(banks[c][:, t, :], 1, t, z_w[:, cols], z_s[:, cols], stop=False)
-                    mm(banks[c][:, t, :], 2, t, z2_w[:], z2_s[:], start=(c == 0))
+        def quantise(words, scales, woven, cols):
+            nc.vector.quantize_mx(out=words[:, cols].bitcast(FP8X4), scales=scales[:, cols], in_=woven.rearrange("p j t -> p (j t)"))
 
-        def finish(c):
-            cols = slice(c * CH, (c + 1) * CH)
-            res[c] = keep.tile([P, PACK, CH], F32, name="res%d" % c)
-            if c == 0:
-                both = keep.tile([P, PACK, CH], F32, name="both")
-                nc.vector.tensor_tensor(out=both[:], in0=banks[c][:], in1=s0[:], op=ADD)
-                nc.vector.tensor_tensor(out=res[c][:], in0=both[:], in1=yh[:, :, cols], op=MULT)
-            elif c == n_ch - 1:
-                for t in range(PACK):
-                    nc.vector.scalar_tensor_tensor(out=res[c][:, t, :], in0=banks[c][t], scalar=2.0, in1=yh[:, t, cols], op0=ADD, op1=MULT)
-            else:
-                nc.vector.scalar_tensor_tensor(out=res[c][:], in0=banks[c][:], scalar=2.0, in1=yh[:, :, cols], op0=ADD, op1=MULT)
-            nc.sync.dma_start(out_rows[:, :, cols], res[c][:])
+        got01 = keep.tile([P, PACK, HALF], BF16, name="got01", align_bytes=64)
+        got2 = keep.tile([P, PACK, CH], BF16, name="got2", align_bytes=64)
+        z2_bf0 = keep.tile([P, HALF, PACK], BF16, name="z2_bf0", tag="z2_bf0", align_bytes=64)
+        z2_bf1 = keep.tile([P, HALF, PACK], BF16, name="z2_bf1", align_bytes=64)
+        fetch(got01, halves[0])
+        for c in range(2):
+            weave(nc.scalar.copy, z2_bf0[:, chunks[c], :], got01[:, :, chunks[c]])
+        fetch(got2, chunks[2])
+        quantise(z2_w, z2_s, z2_bf0[:], halves[0])
+        weave(nc.scalar.copy, z2_bf1[:, chunks[0], :], got2[:])
+        got3 = keep.tile([P, PACK, CH], BF16, name="got3", tag="z2_bf0", align_bytes=64)
+        fetch(got3, chunks[3])
+        weave(nc.scalar.copy, z2_bf1[:, chunks[1], :], got3[:])
 
-        def hand_on(c):
-            cols = slice(c * CH, (c + 1) * CH)
-            o_bf = keep.tile([P, CH, PACK], BF16, name="o_bf%d" % c, align_bytes=64)
-            weave(c, o_bf[:], res[c][:])
-            nc.vector.quantize_mx(out=o_w[:, cols].bitcast(FP8X4), scales=o_s[:, cols], in_=o_bf[:].rearrange("p j t -> p (j t)"))
-            nc.sync.dma_start(out_words[:, cols], o_w[:, cols].bitcast(I32))
+        late = [psum.tile([P, HALF], F32, name="late", tag="b%d" % (4 + t)) for t in range(PACK)]
+        for t in range(PACK):
+            mm(late[t][:], 1, t, z_w[:, halves[1]], z_s[:, halves[1]], stop=False)
+        early = [psum.tile([P, PACK, CH], F32, name="early", tag="b%d" % c) for c in range(2)]
+        for c in range(2):
+            for t in range(PACK):
+                if c == 1:
+                    mm(early[c][:, t, :], 1, t, z_w[:, chunks[c]], z_s[:, chunks[c]], stop=False)
+                mm(early[c][:, t, :], 2, t, z2_w[:, chunks[c]], z2_s[:, chunks[c]], start=(c == 0))
 
-        for step in range(n_ch + 3):
-            if step < n_ch:
-                fetch(step)
-            if 0 <= step - 1 < n_ch:
-                product(step - 1)
-            if 0 <= step - 2 < n_ch:
-                finish(step - 2)
-            if 0 <= step - 3 < n_ch:
-                hand_on(step - 3)
+        res = [keep.tile([P, PACK, HALF], F32, name="res%d" % h) for h in range(2)]
+        o_bf = [keep.tile([P, HALF, PACK], BF16, name="o_bf%d" % h, align_bytes=64) for h in range(2)]
+        both = keep.tile([P, PACK, CH], F32, name="both")
+        nc.vector.tensor_tensor(out=both[:], in0=early[0][:], in1=s0[:], op=ADD)
+        nc.vector.tensor_tensor(out=res[0][:, :, chunks[0]], in0=both[:], in1=yh[:, :, chunks[0]], op=MULT)
+        weave(nc.scalar.copy, o_bf[0][:, chunks[0], :], res[0][:, :, chunks[0]])
+        quantise(z2_w, z2_s, z2_bf1[:], halves[1])
+        for t in range(PACK):
+            mm(late[t][:], 2, t, z2_w[:, halves[1]], z2_s[:, halves[1]], start=False)
+        nc.vector.scalar_tensor_tensor(out=res[0][:, :, chunks[1]], in0=early[1][:], scalar=2.0, in1=yh[:, :, chunks[1]], op0=ADD, op1=MULT)
+        nc.sync.dma_start(out_rows[:, :, halves[0]], res[0][:])
+        weave(nc.scalar.copy, o_bf[0][:, chunks[1], :], res[0][:, :, chunks[1]])
+        for c in range(2):
+            for t in range(PACK):
+                nc.vector.scalar_tensor_tensor(out=res[1][:, t, chunks[c]], in0=late[t][:, chunks[c]], scalar=2.0, in1=yh[:, t, chunks[2 + c]], op0=ADD, op1=MULT)
+            nc.sync.dma_start(out_rows[:, :, chunks[2 + c]], res[1][:, :, chunks[c]])
+            weave(nc.scalar.copy, o_bf[1][:, chunks[c], :], res[1][:, :, chunks[c]])
+        quantise(o_w, o_s, o_bf[0][:], halves[0])
+        nc.sync.dma_start(out_words[:, halves[0]], o_w[:, halves[0]].bitcast(I32))
+        for c in range(2):
+            quantise(o_w, o_s, o_bf[1][:, chunks[c], :], chunks[2 + c])
+        nc.sync.dma_start(out_words[:, halves[1]], o_w[:, halves[1]].bitcast(I32))
         for q in range(4):
-            queue = nc.scalar if q % 2 else nc.sync
+            queue = nc.sync if q == 3 else nc.scalar
             queue.dma_start(out_2[0, 4 * q : 4 * q + 4, :].bitcast(I32), o_s[32 * q : 32 * q + 4, :].bitcast(I32))

@@ -50,8 +50,8 @@ def tile_picked_dcn2_none_po_kernel(
         planes = [keep.tile([P, H], U8, name="plane%d" % i, align_bytes=64) for i in range(3)]
         gain = keep.tile([P, PACK], F32, name="gain")
 
+        nc.vector.memset(raw_s1[:].bitcast(I32), 0)
         nc.vector.memset(xs_all[:].bitcast(I32), 0)
-        nc.gpsimd.memset(raw_s1[:].bitcast(I32), 0)
         nc.vector.memset(xs[:].bitcast(I32), 0)
 
         def load_scale_rows(queue, dst, src):
@@ -114,12 +114,12 @@ def tile_picked_dcn2_none_po_kernel(
         win = [keep.tile([P, S], F32, name="win%d" % t) for t in range(PACK)]
         s0 = keep.tile([P, PACK, CH], F32, name="s0")
         for h in range(2):
-            on_vector = halves[h] if h == 0 else slice(HALF, HALF + CH)
+            on_vector = halves[h] if h == 0 else slice(HALF, S - 64)
             nc.vector.tensor_scalar(out=z_bf[:, on_vector, :].rearrange("p (c i) t -> p c t i", i=4), in0=zh[:, :, on_vector].rearrange("p t (c i) -> p c t i", i=4),
                                     scalar1=2.0, scalar2=None, op0=MULT)
             if h == 1:
-                nc.scalar.activation(z_bf[:, HALF + CH : S, :].rearrange("p (c i) t -> p c t i", i=4),
-                                     zh[:, :, HALF + CH : S].rearrange("p t (c i) -> p c t i", i=4), COPY, scale=2.0)
+                nc.scalar.activation(z_bf[:, S - 64 : S, :].rearrange("p (c i) t -> p c t i", i=4),
+                                     zh[:, :, S - 64 : S].rearrange("p t (c i) -> p c t i", i=4), COPY, scale=2.0)
             nc.vector.quantize_mx(out=z_w[:, halves[h]].bitcast(FP8X4), scales=z_s[:, halves[h]],
                                   in_=z_bf[:, halves[h], :].rearrange("p j t -> p (j t)"))
             for t in range(PACK):
@@ -129,7 +129,7 @@ def tile_picked_dcn2_none_po_kernel(
                 nc.vector.scalar_tensor_tensor(out=win[t][:, halves[h]], in0=m2_ps[h][t // 2][:, t % 2, :], scalar=2.0,
                                                in1=zh[:, t, halves[h]], op0=ADD, op1=MULT)
         for u in range(2):
-            nc.scalar.activation(s0[:, 2 * u : 2 * u + 2, :], m2_ps[0][u][:, :, 0:CH], COPY, bias=2.0)
+            nc.scalar.activation(s0[:, 2 * u : 2 * u + 2, :], m2_ps[0][u][:, :, CH:HALF], COPY, bias=2.0)
         yh = keep.tile([P, PACK, S], F32, name="yh", tag="z_bf", align_bytes=64)
         for h in range(2):
             for u in range(2):
@@ -174,21 +174,22 @@ def tile_picked_dcn2_none_po_kernel(
         early = [psum.tile([P, PACK, CH], F32, name="early", tag="b%d" % c) for c in range(2)]
         for c in range(2):
             for t in range(PACK):
-                if c == 1:
+                if c == 0:
                     mm(early[c][:, t, :], 1, t, z_w[:, chunks[c]], z_s[:, chunks[c]], stop=False)
-                mm(early[c][:, t, :], 2, t, z2_w[:, chunks[c]], z2_s[:, chunks[c]], start=(c == 0))
+                mm(early[c][:, t, :], 2, t, z2_w[:, chunks[c]], z2_s[:, chunks[c]], start=(c == 1))
 
         res = [keep.tile([P, PACK, HALF], F32, name="res%d" % h) for h in range(2)]
         o_bf = [keep.tile([P, HALF, PACK], BF16, name="o_bf%d" % h, align_bytes=64) for h in range(2)]
         both = keep.tile([P, PACK, CH], F32, name="both")
-        nc.vector.tensor_tensor(out=both[:], in0=early[0][:], in1=s0[:], op=ADD)
-        nc.vector.tensor_tensor(out=res[0][:, :, chunks[0]], in0=both[:], in1=yh[:, :, chunks[0]], op=MULT)
+        nc.vector.scalar_tensor_tensor(out=res[0][:, :, chunks[0]], in0=early[0][:], scalar=2.0, in1=yh[:, :, chunks[0]], op0=ADD, op1=MULT)
+        nc.sync.dma_start(out_rows[:, :, chunks[0]], res[0][:, :, chunks[0]])
         weave(nc.scalar.copy, o_bf[0][:, chunks[0], :], res[0][:, :, chunks[0]])
+        nc.vector.tensor_tensor(out=both[:], in0=early[1][:], in1=s0[:], op=ADD)
         quantise(z2_w, z2_s, z2_bf1[:], halves[1])
         for t in range(PACK):
             mm(late[t][:], 2, t, z2_w[:, halves[1]], z2_s[:, halves[1]], start=False)
-        nc.vector.scalar_tensor_tensor(out=res[0][:, :, chunks[1]], in0=early[1][:], scalar=2.0, in1=yh[:, :, chunks[1]], op0=ADD, op1=MULT)
-        nc.sync.dma_start(out_rows[:, :, halves[0]], res[0][:])
+        nc.vector.tensor_tensor(out=res[0][:, :, chunks[1]], in0=both[:], in1=yh[:, :, chunks[1]], op=MULT)
+        nc.sync.dma_start(out_rows[:, :, chunks[1]], res[0][:, :, chunks[1]])
         weave(nc.scalar.copy, o_bf[0][:, chunks[1], :], res[0][:, :, chunks[1]])
         for c in range(2):
             for t in range(PACK):

from contextlib import ExitStack

import concourse.mybir as mybir

F32 = mybir.dt.float32
BF16 = mybir.dt.bfloat16
I32 = mybir.dt.int32
U32 = mybir.dt.uint32
U16 = mybir.dt.uint16
U8 = mybir.dt.uint8
FP8X4 = mybir.dt.float8_e4m3fn_x4
ADD = mybir.AluOpType.add
MULT = mybir.AluOpType.mult
COPY = mybir.ActivationFunctionType.Copy

P = 128
PACK = 4
T, S, H = 2048, 512, 512
HALF = 256
CH = 128
FLOPS = 3 * 2 * 512 * 512 * 512


def tile_picked_dcn2_none_po_kernel(
    tc, x_words, x_scales, w1_words, w1_scales, gn, w2_words, w2_scales, w3_words, w3_scales, offs, pair, out_0, out_1, out_2
):
    nc = tc.nc

    def words_of(ap):
        return ap[0].rearrange("p n t -> p (n t)").bitcast(I32)

    def deal(dst, src, run):
        nc.vector.tensor_copy(out=dst.rearrange("p (t m i) -> p m t i", t=PACK, i=run), in_=src.rearrange("p (m i t) -> p m t i", t=PACK, i=run))

    with ExitStack() as ctx:
        keep = ctx.enter_context(tc.tile_pool(name="keep", bufs=1))
        psum = ctx.enter_context(tc.psum_pool(name="psum", bufs=1))

        offs_t = keep.tile([P, S // 16], U16, name="offs_t")
        pair_t = keep.tile([P, S // 16], U16, name="pair_t")
        xs_all = keep.tile([P, T], U8, name="xs_all", tag="xs_all", align_bytes=64)
        xw_all = keep.tile([P, T], U32, name="xw_all", tag="xw_all", align_bytes=64)
        xs_got = keep.tile([P, S], U8, name="xs_got", tag="xs_got", align_bytes=64)
        xs = keep.tile([P, S], U8, name="xs", align_bytes=64)
        xw = keep.tile([P, S], U32, name="xw", align_bytes=64)
        raw_w = [keep.tile([P, H], I32, name="raw_w%d" % i, tag="raw_w%d" % i, align_bytes=64) for i in range(2)]
        w = {2: keep.tile([P, H], I32, name="w2", align_bytes=64)}
        raw_s1 = keep.tile([P, H], U8, name="raw_s1", align_bytes=64)
        half_gain = keep.tile([P, PACK], F32, name="half_gain")
        planes = [keep.tile([P, H], U8, name="plane%d" % i, align_bytes=64) for i in range(3)]
        gain = keep.tile([P, PACK], F32, name="gain")

        nc.vector.memset(raw_s1[:].bitcast(I32), 0)
        nc.vector.memset(xs_all[:].bitcast(I32), 0)
        nc.vector.memset(xs[:].bitcast(I32), 0)

        def load_scale_rows(queue, dst, src):
            for q in range(4):
                queue.dma_start(dst[32 * q : 32 * q + 4, :].bitcast(I32), src[0, 4 * q : 4 * q + 4, :].bitcast(I32))

        nc.sync.dma_start(offs_t[:], offs)
        nc.sync.dma_start(xs_all[0:P:8, :].bitcast(I32), x_scales[0].bitcast(I32))
        nc.sync.dma_start(raw_w[0][:], words_of(w1_words))
        nc.sync.dma_start(xw_all[:].bitcast(I32), words_of(x_words))
        load_scale_rows(nc.scalar, raw_s1, w1_scales)
        nc.gpsimd.dma_start(gain[:], gn.rearrange("(p t) o -> p (t o)", t=PACK))
        nc.sync.dma_start(pair_t[:], pair)
        nc.sync.dma_start(raw_w[1][:], words_of(w2_words))
        nc.scalar.activation(half_gain[:], gain[:], COPY, scale=0.5)

        nc.vector.tensor_copy(out=xs_got[:], in_=xs_all[:].indirect(offs_t[:]))
        for r in range(4):
            nc.sync.dma_start(xs[r:P:32, :].bitcast(I32), xs_got[8 * r : P : 32, :].bitcast(I32))
        w[0] = keep.tile([P, H], I32, name="w0", tag="xs_all", align_bytes=64)
        deal(w[0][:], raw_w[0][:], 4)
        raw_s2 = keep.tile([P, H], U8, name="raw_s2", tag="raw_w0", align_bytes=64)
        nc.vector.memset(raw_s2[:].bitcast(I32), 0)
        load_scale_rows(nc.sync, raw_s2, w2_scales)
        raw_w3 = keep.tile([P, H], I32, name="raw_w3", tag="xs_got", align_bytes=64)
        nc.sync.dma_start(raw_w3[:], words_of(w3_words))
        deal(planes[0][:], raw_s1[:], 16)
        halves = [slice(h * HALF, (h + 1) * HALF) for h in range(2)]

        def mm(out, i, t, rhs, rhs_scale, start=True, stop=True):
            cols = slice(P * t, P * (t + 1))
            plane = planes[i][:, cols]
            nc.tensor.matmul_mx(out=out, lhsT=w[i][:, cols].bitcast(FP8X4), lhsT_scale=plane,
                                rhs=rhs.bitcast(FP8X4), rhs_scale=rhs_scale, start=start, stop=stop)

        y_ps = [[psum.tile([P, 2, HALF], F32, name="y_ps", tag="b%d" % (2 * h + u)) for u in range(2)] for h in range(2)]
        zh = keep.tile([P, PACK, S], F32, name="zh")
        z_bf = keep.tile([P, S, PACK], BF16, name="z_bf", tag="z_bf", align_bytes=64)
        z_w = keep.tile([P, S], U32, name="z_w", align_bytes=64)
        z_s = keep.tile([P, S], U8, name="z_s", align_bytes=64)

        for h in range(2):
            nc.vector.tensor_copy(out=xw[:, halves[h]], in_=xw_all[:].indirect(offs_t[:, 16 * h : 16 * (h + 1)]))
            for t in range(PACK):
                mm(y_ps[h][t // 2][:, t % 2, :], 0, t, xw[:, halves[h]], xs[:, halves[h]])
        w[1] = keep.tile([P, H], I32, name="w1", tag="xw_all", align_bytes=64)
        deal(w[1][:], raw_w[1][:], 4)
        raw_s3 = keep.tile([P, H], U8, name="raw_s3", tag="raw_w1", align_bytes=64)
        nc.vector.memset(raw_s3[:].bitcast(I32), 0)
        load_scale_rows(nc.sync, raw_s3, w3_scales)
        deal(planes[1][:], raw_s2[:], 16)
        for h in range(2):
            for t in range(PACK):
                src = y_ps[h][t // 2][:, t % 2, :]
                nc.scalar.activation(zh[:, t, halves[h]], src, COPY, scale=half_gain[:, t : t + 1])
        deal(w[2][:], raw_w3[:], 4)
        deal(planes[2][:], raw_s3[:], 16)

        m2_ps = [[psum.tile([P, 2, HALF], F32, name="m2_ps", tag="b%d" % (4 + 2 * h + u)) for u in range(2)] for h in range(2)]
        win = [keep.tile([P, S], F32, name="win%d" % t) for t in range(PACK)]
        s0 = keep.tile([P, PACK, CH], F32, name="s0")
        for h in range(2):
            on_vector = halves[h] if h == 0 else slice(HALF, S - 64)
            nc.vector.tensor_scalar(out=z_bf[:, on_vector, :].rearrange("p (c i) t -> p c t i", i=4), in0=zh[:, :, on_vector].rearrange("p t (c i) -> p c t i", i=4),
                                    scalar1=2.0, scalar2=None, op0=MULT)
            if h == 1:
                nc.scalar.activation(z_bf[:, S - 64 : S, :].rearrange("p (c i) t -> p c t i", i=4),
                                     zh[:, :, S - 64 : S].rearrange("p t (c i) -> p c t i", i=4), COPY, scale=2.0)
            nc.vector.quantize_mx(out=z_w[:, halves[h]].bitcast(FP8X4), scales=z_s[:, halves[h]],
                                  in_=z_bf[:, halves[h], :].rearrange("p j t -> p (j t)"))
            for t in range(PACK):
                mm(m2_ps[h][t // 2][:, t % 2, :], 1, t, z_w[:, halves[h]], z_s[:, halves[h]])
        for h in range(2):
            for t in range(PACK):
                nc.vector.scalar_tensor_tensor(out=win[t][:, halves[h]], in0=m2_ps[h][t // 2][:, t % 2, :], scalar=2.0,
                                               in1=zh[:, t, halves[h]], op0=ADD, op1=MULT)
        for u in range(2):
            nc.scalar.activation(s0[:, 2 * u : 2 * u + 2, :], m2_ps[0][u][:, :, CH:HALF], COPY, bias=2.0)
        yh = keep.tile([P, PACK, S], F32, name="yh", tag="z_bf", align_bytes=64)
        for h in range(2):
            for u in range(2):
                nc.scalar.activation(yh[:, 2 * u : 2 * u + 2, halves[h]], y_ps[h][u][:], COPY, scale=0.5)

        n_ch = S // CH
        o_w = keep.tile([P, S], U32, name="o_w", align_bytes=64)
        o_s = keep.tile([P, S], U8, name="o_s", align_bytes=64)
        out_rows = out_0.rearrange("(p t) j -> p t j", t=PACK)
        out_words = words_of(out_1)
        chunks = [slice(c * CH, (c + 1) * CH) for c in range(n_ch)]
        z2_w = keep.tile([P, S], U32, name="z2_w", align_bytes=64)
        z2_s = keep.tile([P, S], U8, name="z2_s", align_bytes=64)

        def weave(copy, dst, src):
            copy(out=dst.rearrange("p (c i) t -> p c t i", i=4), in_=src.rearrange("p t (c i) -> p c t i", i=4))

        def fetch(got, cols):
            for t in range(PACK):
                nc.vector.tensor_copy(out=got[:, t, :], in_=win[t][:].indirect(pair_t[:, cols.start // 16 : cols.stop // 16]))

        def quantise(words, scales, woven, cols):
            nc.vector.quantize_mx(out=words[:, cols].bitcast(FP8X4), scales=scales[:, cols], in_=woven.rearrange("p j t -> p (j t)"))

        got01 = keep.tile([P, PACK, HALF], BF16, name="got01", align_bytes=64)
        got2 = keep.tile([P, PACK, CH], BF16, name="got2", align_bytes=64)
        z2_bf0 = keep.tile([P, HALF, PACK], BF16, name="z2_bf0", tag="z2_bf0", align_bytes=64)
        z2_bf1 = keep.tile([P, HALF, PACK], BF16, name="z2_bf1", align_bytes=64)
        fetch(got01, halves[0])
        for c in range(2):
            weave(nc.scalar.copy, z2_bf0[:, chunks[c], :], got01[:, :, chunks[c]])
        fetch(got2, chunks[2])
        quantise(z2_w, z2_s, z2_bf0[:], halves[0])
        weave(nc.scalar.copy, z2_bf1[:, chunks[0], :], got2[:])
        got3 = keep.tile([P, PACK, CH], BF16, name="got3", tag="z2_bf0", align_bytes=64)
        fetch(got3, chunks[3])
        weave(nc.scalar.copy, z2_bf1[:, chunks[1], :], got3[:])

        late = [psum.tile([P, HALF], F32, name="late", tag="b%d" % (4 + t)) for t in range(PACK)]
        for t in range(PACK):
            mm(late[t][:], 1, t, z_w[:, halves[1]], z_s[:, halves[1]], stop=False)
        early = [psum.tile([P, PACK, CH], F32, name="early", tag="b%d" % c) for c in range(2)]
        for c in range(2):
            for t in range(PACK):
                if c == 0:
                    mm(early[c][:, t, :], 1, t, z_w[:, chunks[c]], z_s[:, chunks[c]], stop=False)
                mm(early[c][:, t, :], 2, t, z2_w[:, chunks[c]], z2_s[:, chunks[c]], start=(c == 1))

        res = [keep.tile([P, PACK, HALF], F32, name="res%d" % h) for h in range(2)]
        o_bf = [keep.tile([P, HALF, PACK], BF16, name="o_bf%d" % h, align_bytes=64) for h in range(2)]
        both = keep.tile([P, PACK, CH], F32, name="both")
        nc.vector.scalar_tensor_tensor(out=res[0][:, :, chunks[0]], in0=early[0][:], scalar=2.0, in1=yh[:, :, chunks[0]], op0=ADD, op1=MULT)
        nc.sync.dma_start(out_rows[:, :, chunks[0]], res[0][:, :, chunks[0]])
        weave(nc.scalar.copy, o_bf[0][:, chunks[0], :], res[0][:, :, chunks[0]])
        nc.vector.tensor_tensor(out=both[:], in0=early[1][:], in1=s0[:], op=ADD)
        quantise(z2_w, z2_s, z2_bf1[:], halves[1])
        for t in range(PACK):
            mm(late[t][:], 2, t, z2_w[:, halves[1]], z2_s[:, halves[1]], start=False)
        nc.vector.tensor_tensor(out=res[0][:, :, chunks[1]], in0=both[:], in1=yh[:, :, chunks[1]], op=MULT)
        nc.sync.dma_start(out_rows[:, :, chunks[1]], res[0][:, :, chunks[1]])
        weave(nc.scalar.copy, o_bf[0][:, chunks[1], :], res[0][:, :, chunks[1]])
        for c in range(2):
            for t in range(PACK):
                nc.vector.scalar_tensor_tensor(out=res[1][:, t, chunks[c]], in0=late[t][:, chunks[c]], scalar=2.0, in1=yh[:, t, chunks[2 + c]], op0=ADD, op1=MULT)
            nc.sync.dma_start(out_rows[:, :, chunks[2 + c]], res[1][:, :, chunks[c]])
            weave(nc.scalar.copy, o_bf[1][:, chunks[c], :], res[1][:, :, chunks[c]])
        quantise(o_w, o_s, o_bf[0][:], halves[0])
        nc.sync.dma_start(out_words[:, halves[0]], o_w[:, halves[0]].bitcast(I32))
        for c in range(2):
            quantise(o_w, o_s, o_bf[1][:, chunks[c], :], chunks[2 + c])
        nc.sync.dma_start(out_words[:, halves[1]], o_w[:, halves[1]].bitcast(I32))
        for q in range(4):
            queue = nc.sync if q == 3 else nc.scalar
            queue.dma_start(out_2[0, 4 * q : 4 * q + 4, :].bitcast(I32), o_s[32 * q : 32 * q + 4, :].bitcast(I32))
